import numpy as np
import ml_dtypes


def mxq(x, axis, fmt="e4m3"):
    dtype, down = {"e4m3": (ml_dtypes.float8_e4m3fn, 7), "e5m2": (ml_dtypes.float8_e5m2, 14)}[fmt]
    v = np.moveaxis(np.asarray(x, np.float32).astype(ml_dtypes.bfloat16).astype(np.float64), axis, -1)
    blocks = v.reshape(v.shape[:-1] + (-1, 32))
    amax = np.abs(blocks).max(-1, keepdims=True)
    byte = np.maximum(np.where(amax > 0, np.frexp(amax)[1] - 1 + 127, 0) - down, 1)
    scale = np.exp2(byte - 127.0)
    codes = (blocks / scale).astype(np.float32).astype(dtype).astype(np.float64)
    return np.moveaxis((codes * scale).reshape(v.shape), -1, axis)


WIDE = False


def mx_kscale(k):
    if not WIDE:
        return np.ones(k)
    levels = np.array([30, -30])
    if k % 512:
        return np.exp2(np.random.permutation(np.resize(levels, k // 32))).repeat(32)
    a = np.empty((k // 512, 16))
    for p in range(k // 512):
        a[p, :8] = np.random.permutation(np.resize(levels, 8))
        for g in range(8):
            far = levels[np.abs(levels - a[p, g]) >= 10]
            a[p, g + 8] = far[np.random.randint(len(far))]
    return np.exp2(a.ravel()).repeat(32)


def f64(x):
    return np.asarray(x).astype(np.float64)


def striped(idx):
    return np.tile(np.asarray(idx).reshape(-1, 16).T, (8, 1)).astype(np.uint16)


def unstriped(offs):
    return offs[:16].T.reshape(-1).astype(np.int64)


E2M1 = np.array([0.0, 0.5, 1.0, 1.5, 2.0, 3.0, 4.0, 6.0, -0.0, -0.5, -1.0, -1.5, -2.0, -3.0, -4.0, -6.0])


def pack_weight(w, fmt):
    k, n = w.shape
    w = f64(np.asarray(w, np.float32).astype(ml_dtypes.bfloat16)).reshape(k // 32, 32, n)
    amax = np.abs(w).max(1)
    if fmt in ("e4m3", "e5m2"):
        byte = np.frexp(amax)[1] - 1 + 127 - (7 if fmt == "e4m3" else 14)
    else:
        mant, ex = np.frexp(amax / 6.0)
        byte = np.where(mant > 0.5, ex, ex - 1) + 127
    byte = np.clip(np.where(amax > 0, byte, 1), 1, 254)
    scaled = (w * np.exp2(127.0 - byte)[:, None, :]).reshape(k, n).astype(np.float32)
    by_word = np.ascontiguousarray(scaled.reshape(k // 512, 128, 4, n).transpose(0, 1, 3, 2))
    if fmt in ("e4m3", "e5m2"):
        words = by_word.astype(ml_dtypes.float8_e4m3fn if fmt == "e4m3" else ml_dtypes.float8_e5m2).view(np.uint8)
    else:
        c = by_word.astype(ml_dtypes.float4_e2m1fn).view(np.uint8) & 0xF
        words = (c[..., 0::2] | (c[..., 1::2] << 4)).reshape(k // 512, 128, 2 * n)
    return np.ascontiguousarray(words), np.ascontiguousarray(byte.astype(np.uint8).reshape(k // 512, 16, n))


def unpack_weight(words, scales, fmt):
    g, _, n = scales.shape
    words = np.ascontiguousarray(words).reshape(g, 128, n, -1)
    if fmt in ("e4m3", "e5m2"):
        vals = words.view(ml_dtypes.float8_e4m3fn if fmt == "e4m3" else ml_dtypes.float8_e5m2).astype(np.float64)
    else:
        nib = np.empty((g, 128, n, 4), np.uint8)
        nib[..., 0::2] = words & 0xF
        nib[..., 1::2] = words >> 4
        vals = E2M1[nib]
    vals = vals * np.repeat(np.exp2(scales.astype(np.float64) - 127.0), 8, axis=1)[..., None]
    return vals.transpose(0, 1, 3, 2).reshape(g * 512, n)


K, T, I, J, N, Z, S, V, O, E = 512, 1024, 512, 256, 256, 1024, 1024, 1024, 128, 1024


def setup_inputs():
    n = np.random.standard_normal
    idx = np.random.permutation(T)[:I]
    idx2 = np.random.permutation(Z)[:J]
    idx3 = np.random.permutation(V)[:J]
    idx4 = np.random.permutation(J)[:O]
    idx5 = np.random.permutation(J)[:O]
    idx6 = np.random.permutation(S)[:N]
    idx7 = np.random.permutation(E)[:O]
    fk = mx_kscale(K)
    fi = mx_kscale(I)
    ti = np.ones(T)
    ti[idx] = fi
    xkp = pack_weight(n((K, T)) * 0.3 * fk[:, None] * ti, "e2m1")
    xqp = pack_weight(n((K, Z)) * 0.3 / fk[:, None], "e4m3")
    xrp = pack_weight(n((K, V)) * 0.3 / fk[:, None], "e5m2")
    vsp = pack_weight(n((I, S)) / fi[:, None], "e4m3")
    return {
        "xk_words": xkp[0],
        "xk_scales": xkp[1],
        "xq_words": xqp[0],
        "xq_scales": xqp[1],
        "xr_words": xrp[0],
        "xr_scales": xrp[1],
        "vs_words": vsp[0],
        "vs_scales": vsp[1],
        "offs": striped(idx),
        "offs2": striped(idx2),
        "offs3": striped(idx3),
        "offs4": striped(idx4),
        "offs5": striped(idx5),
        "offs6": striped(idx6),
        "offs7": striped(idx7),
    }


def reference(xk_words, xk_scales, xq_words, xq_scales, xr_words, xr_scales, vs_words, vs_scales, offs, offs2, offs3, offs4, offs5, offs6, offs7):
    idx = unstriped(offs)
    idx2 = unstriped(offs2)
    idx3 = unstriped(offs3)
    idx4 = unstriped(offs4)
    idx5 = unstriped(offs5)
    idx6 = unstriped(offs6)
    idx7 = unstriped(offs7)
    xku = unpack_weight(xk_words, xk_scales, "e2m1")
    xqu = unpack_weight(xq_words, xq_scales, "e4m3")
    xru = unpack_weight(xr_words, xr_scales, "e5m2")
    vsu = unpack_weight(vs_words, vs_scales, "e4m3")
    xkidxg = xku[:, idx]
    xqidx2g = xqu[:, idx2]
    s1 = xkidxg.T @ xqidx2g
    xridx3g = xru[:, idx3]
    s2 = xkidxg.T @ xridx3g
    hid = np.maximum(s1[:, idx4] - s2[:, idx5], 0.0)
    vsidx6g = vsu[:, idx6]
    hidq = mxq(hid, 0, "e5m2")
    p = vsidx6g.T @ hidq
    y = np.zeros((N, E))
    y[:, idx7] = p
    return y

@@ -1,0 +1,160 @@
+from contextlib import ExitStack
+
+import concourse.mybir as mybir
+
+F32 = mybir.dt.float32
+BF16 = mybir.dt.bfloat16
+I32 = mybir.dt.int32
+U32 = mybir.dt.uint32
+U16 = mybir.dt.uint16
+U8 = mybir.dt.uint8
+E2M1 = mybir.dt.float4_e2m1fn_x4
+E4M3 = mybir.dt.float8_e4m3fn_x4
+E5M2 = mybir.dt.float8_e5m2_x4
+COPY = mybir.ActivationFunctionType.Copy
+SUBTRACT = mybir.AluOpType.subtract
+
+P = 128
+PACK = 4
+TABLE = 1024
+ROWS = 512
+COLS = 256
+FEATS = 256
+PLACES = 128
+PAGE = 1024
+
+FLOPS = 2 * 512 * ROWS * COLS * 2 + 2 * ROWS * FEATS * PLACES
+
+
+def tile_list_contest_rivals_looked_scattered_kernel(
+    tc, xk_words, xk_scales, xq_words, xq_scales, xr_words, xr_scales, vs_words, vs_scales,
+    offs, offs2, offs3, offs4, offs5, offs6, offs7, out,
+):
+    nc = tc.nc
+    with ExitStack() as ctx:
+        sb = ctx.enter_context(tc.tile_pool(name="sb", bufs=1))
+        ps = ctx.enter_context(tc.psum_pool(name="ps", bufs=1))
+
+        def load_list(src, name):
+            tile = sb.tile(list(src.shape), U16, name=name)
+            nc.sync.dma_start(tile[:], src)
+            return tile
+
+        def zeroed_scale_table(name):
+            tile = sb.tile([P, TABLE], U8, name=name)
+            nc.vector.memset(tile[:].bitcast(I32), 0)
+            return tile
+
+        def load_scales(tile, src):
+            for r in range(4):
+                nc.sync.dma_start(tile[r:P:32, :].bitcast(I32), src[0, r:16:4, :].bitcast(I32))
+
+        def load_words(src, name):
+            tile = sb.tile([P, TABLE], U32, name=name)
+            nc.sync.dma_start(tile[:].bitcast(I32), src[0].rearrange("p n t -> p (n t)").bitcast(I32))
+            return tile
+
+        def gather(table, offsets, count, dtype, name):
+            tile = sb.tile([P, count], dtype, name=name, align_bytes=64)
+            nc.vector.tensor_copy(tile[:], table[:].indirect(offsets[:]))
+            return tile
+
+        k_scale_table = zeroed_scale_table("k_scale_table")
+        r_scale_table = zeroed_scale_table("r_scale_table")
+        q_scale_table = zeroed_scale_table("q_scale_table")
+        v_scale_table = zeroed_scale_table("v_scale_table")
+        pages = [sb.tile([P, PAGE], F32, name=f"page{h}") for h in range(FEATS // P)]
+        for page in pages:
+            nc.vector.memset(page[:], 0.0)
+
+        k_list = load_list(offs, "k_list")
+        k_word_table = sb.tile([P, TABLE], U16, name="k_word_table")
+        nc.sync.dma_start(k_word_table[:].bitcast(I32), xk_words[0].bitcast(I32))
+        load_scales(k_scale_table, xk_scales)
+        r_list = load_list(offs3, "r_list")
+        r_word_table = load_words(xr_words, "r_word_table")
+        load_scales(r_scale_table, xr_scales)
+        q_list = load_list(offs2, "q_list")
+        q_word_table = load_words(xq_words, "q_word_table")
+        load_scales(q_scale_table, xq_scales)
+        s2_list = load_list(offs5, "s2_list")
+        s1_list = load_list(offs4, "s1_list")
+        v_list = load_list(offs6, "v_list")
+        v_word_table = load_words(vs_words, "v_word_table")
+        load_scales(v_scale_table, vs_scales)
+        page_list = load_list(offs7, "page_list")
+
+        k_listed = gather(k_word_table, k_list, ROWS, U16, "k_listed")
+        k_scales = sb.tile([P, ROWS], U8, name="k_scales", align_bytes=64)
+        nc.vector.tensor_copy(
+            k_scales[:].rearrange("p (t m) -> p m t", t=PACK), k_scale_table[:].indirect(k_list[:])
+        )
+        k_words = sb.tile([P, ROWS], U16, name="k_words", align_bytes=64)
+        nc.vector.tensor_copy(
+            k_words[:].rearrange("p (t c i) -> p c t i", t=PACK, i=8),
+            k_listed[:].rearrange("p (c i t) -> p c t i", t=PACK, i=8),
+        )
+
+        def scores(dst, t, words, scales, fmt):
+            cols = slice(t * P, (t + 1) * P)
+            nc.tensor.matmul_mx(
+                out=dst, lhsT=k_words[:, cols].bitcast(E2M1), lhsT_scale=k_scales[:, cols],
+                rhs=words[:].bitcast(fmt), rhs_scale=scales[:], start=True, stop=True,
+            )
+
+        r_words = gather(r_word_table, r_list, COLS, U32, "r_words")
+        r_scales = gather(r_scale_table, r_list, COLS, U8, "r_scales")
+        s2_banks = [ps.tile([P, 2 * COLS], F32, name=f"s2_bank{b}") for b in range(2)]
+        for t in range(PACK):
+            scores(s2_banks[t // 2][:, (t % 2) * COLS : (t % 2 + 1) * COLS], t, r_words, r_scales, E5M2)
+
+        q_words = gather(q_word_table, q_list, COLS, U32, "q_words")
+        q_scales = gather(q_scale_table, q_list, COLS, U8, "q_scales")
+        s1_banks = [ps.tile([P, COLS], F32, name=f"s1_bank{t}") for t in range(PACK)]
+        for t in range(PACK):
+            scores(s1_banks[t][:], t, q_words, q_scales, E4M3)
+
+        v_words = gather(v_word_table, v_list, FEATS, U32, "v_words")
+        v_scales = gather(v_scale_table, v_list, FEATS, U8, "v_scales")
+
+        margin = sb.tile([P, PACK, PLACES], F32, name="margin")
+        for b in range(2):
+            s2 = sb.tile([P, 2 * COLS], F32, name=f"s2_{b}")
+            nc.scalar.copy(s2[:], s2_banks[b][:])
+            for t in (2 * b, 2 * b + 1):
+                s2_listed = sb.tile([P, PLACES], F32, name=f"s2_listed{t}")
+                nc.scalar.activation(
+                    s2_listed[:], s2[:, (t % 2) * COLS : (t % 2 + 1) * COLS].indirect(s2_list[:]), COPY
+                )
+                s1 = sb.tile([P, COLS], F32, name=f"s1_{t}")
+                nc.scalar.copy(s1[:], s1_banks[t][:])
+                nc.vector.tensor_tensor(margin[:, t, :], s1[:].indirect(s1_list[:]), s2_listed[:], SUBTRACT)
+
+        hid = sb.tile([P, PLACES, PACK], BF16, name="hid", align_bytes=64)
+        nc.vector.tensor_scalar_max(
+            hid[:].rearrange("p (c i) t -> p c t i", i=4),
+            margin[:].rearrange("p t (c i) -> p c t i", i=4),
+            0.0,
+        )
+        hid_words = sb.tile([P, PLACES], U32, name="hid_words", align_bytes=64)
+        hid_scales = sb.tile([P, PLACES], U8, name="hid_scales", align_bytes=64)
+        nc.vector.quantize_mx(
+            out=hid_words[:].bitcast(E5M2), scales=hid_scales[:], in_=hid[:].rearrange("p o t -> p (o t)")
+        )
+
+        for h, page in enumerate(pages):
+            cols = slice(h * P, (h + 1) * P)
+            bank = ps.tile([P, PLACES], F32, name=f"p_bank{h}")
+            nc.tensor.matmul_mx(
+                out=bank[:], lhsT=v_words[:, cols].bitcast(E4M3), lhsT_scale=v_scales[:, cols],
+                rhs=hid_words[:].bitcast(E5M2), rhs_scale=hid_scales[:], start=True, stop=True,
+            )
+            product = sb.tile([P, PLACES], F32, name=f"product{h}")
+            if h == 0:
+                nc.vector.tensor_copy(product[:], bank[:])
+                nc.vector.tensor_copy(page[:].indirect(page_list[:]), product[:])
+                nc.sync.dma_start(out[cols, :], page[:])
+            else:
+                nc.scalar.copy(product[:], bank[:])
+                nc.scalar.activation(page[:].indirect(page_list[:]), product[:], COPY)
+                nc.scalar.dma_start(out[cols, :], page[:])

@@ -33,6 +33,7 @@ def tile_list_contest_rivals_looked_scattered_kernel(
     nc = tc.nc
     with ExitStack() as ctx:
         sb = ctx.enter_context(tc.tile_pool(name="sb", bufs=1))
+        reused = ctx.enter_context(tc.tile_pool(name="reused", bufs=1))
         ps = ctx.enter_context(tc.psum_pool(name="ps", bufs=1))
 
         def load_list(src, name):
@@ -49,8 +50,7 @@ def tile_list_contest_rivals_looked_scattered_kernel(
             for r in range(4):
                 nc.sync.dma_start(tile[r:P:32, :].bitcast(I32), src[0, r:16:4, :].bitcast(I32))
 
-        def load_words(src, name):
-            tile = sb.tile([P, TABLE], U32, name=name)
+        def load_words(src, tile):
             nc.sync.dma_start(tile[:].bitcast(I32), src[0].rearrange("p n t -> p (n t)").bitcast(I32))
             return tile
 
@@ -65,22 +65,22 @@ def tile_list_contest_rivals_looked_scattered_kernel(
         v_scale_table = zeroed_scale_table("v_scale_table")
         pages = [sb.tile([P, PAGE], F32, name=f"page{h}") for h in range(FEATS // P)]
         for page in pages:
-            nc.vector.memset(page[:], 0.0)
+            nc.vector.memset(page[:].bitcast(I32), 0)
 
-        k_list = load_list(offs, "k_list")
         k_word_table = sb.tile([P, TABLE], U16, name="k_word_table")
         nc.sync.dma_start(k_word_table[:].bitcast(I32), xk_words[0].bitcast(I32))
+        k_list = load_list(offs, "k_list")
         load_scales(k_scale_table, xk_scales)
         r_list = load_list(offs3, "r_list")
-        r_word_table = load_words(xr_words, "r_word_table")
+        r_word_table = load_words(xr_words, sb.tile([P, TABLE], U32, name="r_word_table"))
         load_scales(r_scale_table, xr_scales)
         q_list = load_list(offs2, "q_list")
-        q_word_table = load_words(xq_words, "q_word_table")
+        q_word_table = load_words(xq_words, sb.tile([P, TABLE], U32, name="q_word_table"))
         load_scales(q_scale_table, xq_scales)
+        v_list = load_list(offs6, "v_list")
+        v_word_table = load_words(vs_words, reused.tile([P, TABLE], U32, name="v_word_table", offset=0))
         s2_list = load_list(offs5, "s2_list")
         s1_list = load_list(offs4, "s1_list")
-        v_list = load_list(offs6, "v_list")
-        v_word_table = load_words(vs_words, "v_word_table")
         load_scales(v_scale_table, vs_scales)
         page_list = load_list(offs7, "page_list")
 
@@ -104,9 +104,11 @@ def tile_list_contest_rivals_looked_scattered_kernel(
 
         r_words = gather(r_word_table, r_list, COLS, U32, "r_words")
         r_scales = gather(r_scale_table, r_list, COLS, U8, "r_scales")
-        s2_banks = [ps.tile([P, 2 * COLS], F32, name=f"s2_bank{b}") for b in range(2)]
-        for t in range(PACK):
-            scores(s2_banks[t // 2][:, (t % 2) * COLS : (t % 2 + 1) * COLS], t, r_words, r_scales, E5M2)
+        s2_groups = [(0,), (1,), (2, 3)]
+        s2_banks = [ps.tile([P, len(g) * COLS], F32, name=f"s2_bank{g[0]}") for g in s2_groups]
+        for group, bank in zip(s2_groups, s2_banks):
+            for n, t in enumerate(group):
+                scores(bank[:, n * COLS : (n + 1) * COLS], t, r_words, r_scales, E5M2)
 
         q_words = gather(q_word_table, q_list, COLS, U32, "q_words")
         q_scales = gather(q_scale_table, q_list, COLS, U8, "q_scales")
@@ -117,18 +119,27 @@ def tile_list_contest_rivals_looked_scattered_kernel(
         v_words = gather(v_word_table, v_list, FEATS, U32, "v_words")
         v_scales = gather(v_scale_table, v_list, FEATS, U8, "v_scales")
 
-        margin = sb.tile([P, PACK, PLACES], F32, name="margin")
-        for b in range(2):
-            s2 = sb.tile([P, 2 * COLS], F32, name=f"s2_{b}")
-            nc.scalar.copy(s2[:], s2_banks[b][:])
-            for t in (2 * b, 2 * b + 1):
-                s2_listed = sb.tile([P, PLACES], F32, name=f"s2_listed{t}")
-                nc.scalar.activation(
-                    s2_listed[:], s2[:, (t % 2) * COLS : (t % 2 + 1) * COLS].indirect(s2_list[:]), COPY
-                )
-                s1 = sb.tile([P, COLS], F32, name=f"s1_{t}")
-                nc.scalar.copy(s1[:], s1_banks[t][:])
-                nc.vector.tensor_tensor(margin[:, t, :], s1[:].indirect(s1_list[:]), s2_listed[:], SUBTRACT)
+        margin = sb.tile([P, PACK, PLACES], F32, name="margin", tag="v_scale_table")
+        s1 = [reused.tile([P, COLS], F32, name=f"s1_{t}", offset=t * COLS * 4) for t in range(PACK)]
+        s2 = [sb.tile([P, len(g) * COLS], F32, name=f"s2_{g[0]}") for g in s2_groups]
+        s2_windows = [s2[0][:], s2[1][:], s2[2][:, :COLS], s2[2][:, COLS:]]
+        s2_listed = [sb.tile([P, PLACES], F32, name=f"s2_listed{t}") for t in range(PACK)]
+
+        def pick_s2(t):
+            nc.scalar.activation(s2_listed[t][:], s2_windows[t].indirect(s2_list[:]), COPY)
+
+        nc.scalar.copy(s2[0][:], s2_banks[0][:])
+        nc.scalar.copy(s2[1][:], s2_banks[1][:])
+        pick_s2(0)
+        pick_s2(1)
+        nc.scalar.copy(s2[2][:], s2_banks[2][:])
+        for t in (2, 3):
+            nc.scalar.copy(s1[t][:], s1_banks[t][:])
+            pick_s2(t)
+        for t in (0, 1):
+            nc.vector.tensor_copy(s1[t][:], s1_banks[t][:])
+        for t in range(PACK):
+            nc.vector.tensor_tensor(margin[:, t, :], s1[t][:].indirect(s1_list[:]), s2_listed[t][:], SUBTRACT)
 
         hid = sb.tile([P, PLACES, PACK], BF16, name="hid", align_bytes=64)
         nc.vector.tensor_scalar_max(
@@ -144,7 +155,7 @@ def tile_list_contest_rivals_looked_scattered_kernel(
 
         for h, page in enumerate(pages):
             cols = slice(h * P, (h + 1) * P)
-            bank = ps.tile([P, PLACES], F32, name=f"p_bank{h}")
+            bank = ps.tile([P, PLACES], F32, name=f"p_bank{h}", tag=f"s2_bank{h}")
             nc.tensor.matmul_mx(
                 out=bank[:], lhsT=v_words[:, cols].bitcast(E4M3), lhsT_scale=v_scales[:, cols],
                 rhs=hid_words[:].bitcast(E5M2), rhs_scale=hid_scales[:], start=True, stop=True,

from contextlib import ExitStack

import concourse.mybir as mybir

F32 = mybir.dt.float32
BF16 = mybir.dt.bfloat16
I32 = mybir.dt.int32
U32 = mybir.dt.uint32
U16 = mybir.dt.uint16
U8 = mybir.dt.uint8
E2M1 = mybir.dt.float4_e2m1fn_x4
E4M3 = mybir.dt.float8_e4m3fn_x4
E5M2 = mybir.dt.float8_e5m2_x4
COPY = mybir.ActivationFunctionType.Copy
SUBTRACT = mybir.AluOpType.subtract

P = 128
PACK = 4
TABLE = 1024
ROWS = 512
COLS = 256
FEATS = 256
PLACES = 128
PAGE = 1024

FLOPS = 2 * 512 * ROWS * COLS * 2 + 2 * ROWS * FEATS * PLACES


def tile_list_contest_rivals_looked_scattered_kernel(
    tc, xk_words, xk_scales, xq_words, xq_scales, xr_words, xr_scales, vs_words, vs_scales,
    offs, offs2, offs3, offs4, offs5, offs6, offs7, out,
):
    nc = tc.nc
    with ExitStack() as ctx:
        sb = ctx.enter_context(tc.tile_pool(name="sb", bufs=1))
        reused = ctx.enter_context(tc.tile_pool(name="reused", bufs=1))
        ps = ctx.enter_context(tc.psum_pool(name="ps", bufs=1))

        def load_list(src, name):
            tile = sb.tile(list(src.shape), U16, name=name)
            nc.sync.dma_start(tile[:], src)
            return tile

        def zeroed_scale_table(name):
            tile = sb.tile([P, TABLE], U8, name=name)
            nc.vector.memset(tile[:].bitcast(I32), 0)
            return tile

        def load_scales(tile, src):
            for r in range(4):
                nc.sync.dma_start(tile[r:P:32, :].bitcast(I32), src[0, r:16:4, :].bitcast(I32))

        def load_words(src, tile):
            nc.sync.dma_start(tile[:].bitcast(I32), src[0].rearrange("p n t -> p (n t)").bitcast(I32))
            return tile

        def gather(table, offsets, count, dtype, name):
            tile = sb.tile([P, count], dtype, name=name, align_bytes=64)
            nc.vector.tensor_copy(tile[:], table[:].indirect(offsets[:]))
            return tile

        k_scale_table = zeroed_scale_table("k_scale_table")
        r_scale_table = zeroed_scale_table("r_scale_table")
        q_scale_table = zeroed_scale_table("q_scale_table")
        v_scale_table = zeroed_scale_table("v_scale_table")
        pages = [sb.tile([P, PAGE], F32, name=f"page{h}") for h in range(FEATS // P)]
        for page in pages:
            nc.vector.memset(page[:].bitcast(I32), 0)

        k_word_table = sb.tile([P, TABLE], U16, name="k_word_table")
        nc.sync.dma_start(k_word_table[:].bitcast(I32), xk_words[0].bitcast(I32))
        k_list = load_list(offs, "k_list")
        load_scales(k_scale_table, xk_scales)
        r_list = load_list(offs3, "r_list")
        r_word_table = load_words(xr_words, sb.tile([P, TABLE], U32, name="r_word_table"))
        load_scales(r_scale_table, xr_scales)
        q_list = load_list(offs2, "q_list")
        q_word_table = load_words(xq_words, sb.tile([P, TABLE], U32, name="q_word_table"))
        load_scales(q_scale_table, xq_scales)
        v_list = load_list(offs6, "v_list")
        v_word_table = load_words(vs_words, reused.tile([P, TABLE], U32, name="v_word_table", offset=0))
        s2_list = load_list(offs5, "s2_list")
        s1_list = load_list(offs4, "s1_list")
        load_scales(v_scale_table, vs_scales)
        page_list = load_list(offs7, "page_list")

        k_listed = gather(k_word_table, k_list, ROWS, U16, "k_listed")
        k_scales = sb.tile([P, ROWS], U8, name="k_scales", align_bytes=64)
        nc.vector.tensor_copy(
            k_scales[:].rearrange("p (t m) -> p m t", t=PACK), k_scale_table[:].indirect(k_list[:])
        )
        k_words = sb.tile([P, ROWS], U16, name="k_words", align_bytes=64)
        nc.vector.tensor_copy(
            k_words[:].rearrange("p (t c i) -> p c t i", t=PACK, i=8),
            k_listed[:].rearrange("p (c i t) -> p c t i", t=PACK, i=8),
        )

        def scores(dst, t, words, scales, fmt):
            cols = slice(t * P, (t + 1) * P)
            nc.tensor.matmul_mx(
                out=dst, lhsT=k_words[:, cols].bitcast(E2M1), lhsT_scale=k_scales[:, cols],
                rhs=words[:].bitcast(fmt), rhs_scale=scales[:], start=True, stop=True,
            )

        r_words = gather(r_word_table, r_list, COLS, U32, "r_words")
        r_scales = gather(r_scale_table, r_list, COLS, U8, "r_scales")
        s2_groups = [(0,), (1,), (2, 3)]
        s2_banks = [ps.tile([P, len(g) * COLS], F32, name=f"s2_bank{g[0]}") for g in s2_groups]
        for group, bank in zip(s2_groups, s2_banks):
            for n, t in enumerate(group):
                scores(bank[:, n * COLS : (n + 1) * COLS], t, r_words, r_scales, E5M2)

        q_words = gather(q_word_table, q_list, COLS, U32, "q_words")
        q_scales = gather(q_scale_table, q_list, COLS, U8, "q_scales")
        s1_banks = [ps.tile([P, COLS], F32, name=f"s1_bank{t}") for t in range(PACK)]
        for t in range(PACK):
            scores(s1_banks[t][:], t, q_words, q_scales, E4M3)

        v_words = gather(v_word_table, v_list, FEATS, U32, "v_words")
        v_scales = gather(v_scale_table, v_list, FEATS, U8, "v_scales")

        margin = sb.tile([P, PACK, PLACES], F32, name="margin", tag="v_scale_table")
        s1 = [reused.tile([P, COLS], F32, name=f"s1_{t}", offset=t * COLS * 4) for t in range(PACK)]
        s2 = [sb.tile([P, len(g) * COLS], F32, name=f"s2_{g[0]}") for g in s2_groups]
        s2_windows = [s2[0][:], s2[1][:], s2[2][:, :COLS], s2[2][:, COLS:]]
        s2_listed = [sb.tile([P, PLACES], F32, name=f"s2_listed{t}") for t in range(PACK)]

        def pick_s2(t):
            nc.scalar.activation(s2_listed[t][:], s2_windows[t].indirect(s2_list[:]), COPY)

        nc.scalar.copy(s2[0][:], s2_banks[0][:])
        nc.scalar.copy(s2[1][:], s2_banks[1][:])
        pick_s2(0)
        pick_s2(1)
        nc.scalar.copy(s2[2][:], s2_banks[2][:])
        for t in (2, 3):
            nc.scalar.copy(s1[t][:], s1_banks[t][:])
            pick_s2(t)
        for t in (0, 1):
            nc.vector.tensor_copy(s1[t][:], s1_banks[t][:])
        for t in range(PACK):
            nc.vector.tensor_tensor(margin[:, t, :], s1[t][:].indirect(s1_list[:]), s2_listed[t][:], SUBTRACT)

        hid = sb.tile([P, PLACES, PACK], BF16, name="hid", align_bytes=64)
        nc.vector.tensor_scalar_max(
            hid[:].rearrange("p (c i) t -> p c t i", i=4),
            margin[:].rearrange("p t (c i) -> p c t i", i=4),
            0.0,
        )
        hid_words = sb.tile([P, PLACES], U32, name="hid_words", align_bytes=64)
        hid_scales = sb.tile([P, PLACES], U8, name="hid_scales", align_bytes=64)
        nc.vector.quantize_mx(
            out=hid_words[:].bitcast(E5M2), scales=hid_scales[:], in_=hid[:].rearrange("p o t -> p (o t)")
        )

        for h, page in enumerate(pages):
            cols = slice(h * P, (h + 1) * P)
            bank = ps.tile([P, PLACES], F32, name=f"p_bank{h}", tag=f"s2_bank{h}")
            nc.tensor.matmul_mx(
                out=bank[:], lhsT=v_words[:, cols].bitcast(E4M3), lhsT_scale=v_scales[:, cols],
                rhs=hid_words[:].bitcast(E5M2), rhs_scale=hid_scales[:], start=True, stop=True,
            )
            product = sb.tile([P, PLACES], F32, name=f"product{h}")
            if h == 0:
                nc.vector.tensor_copy(product[:], bank[:])
                nc.vector.tensor_copy(page[:].indirect(page_list[:]), product[:])
                nc.sync.dma_start(out[cols, :], page[:])
            else:
                nc.scalar.copy(product[:], bank[:])
                nc.scalar.activation(page[:].indirect(page_list[:]), product[:], COPY)
                nc.scalar.dma_start(out[cols, :], page[:])
